import numpy as np
import ml_dtypes


def mxq(x, axis, fmt="e4m3"):
    dtype, down = {"e4m3": (ml_dtypes.float8_e4m3fn, 7), "e5m2": (ml_dtypes.float8_e5m2, 14)}[fmt]
    v = np.moveaxis(np.asarray(x, np.float32).astype(ml_dtypes.bfloat16).astype(np.float64), axis, -1)
    blocks = v.reshape(v.shape[:-1] + (-1, 32))
    amax = np.abs(blocks).max(-1, keepdims=True)
    byte = np.maximum(np.where(amax > 0, np.frexp(amax)[1] - 1 + 127, 0) - down, 1)
    scale = np.exp2(byte - 127.0)
    codes = (blocks / scale).astype(np.float32).astype(dtype).astype(np.float64)
    return np.moveaxis((codes * scale).reshape(v.shape), -1, axis)


WIDE = False


def mx_kscale(k, group=512):
    if not WIDE:
        return np.ones(k)
    levels = np.array([18, -18])
    if group != 512:
        return np.exp2(np.random.permutation(np.resize(levels, k // group))).repeat(group)
    if k % 512:
        return np.exp2(np.random.permutation(np.resize(levels, k // 32))).repeat(32)
    a = np.empty((k // 512, 16))
    for p in range(k // 512):
        a[p, :8] = np.random.permutation(np.resize(levels, 8))
        for g in range(8):
            far = levels[np.abs(levels - a[p, g]) >= 10]
            a[p, g + 8] = far[np.random.randint(len(far))]
    return np.exp2(a.ravel()).repeat(32)


def f64(x):
    return np.asarray(x).astype(np.float64)


H, D, N = 8, 128, 512


def setup_inputs():
    n = np.random.standard_normal
    s = mx_kscale(D, 0)
    u = mx_kscale(N)
    t = np.random.uniform(0.5, 2.0, N) * u
    v = n((H, N, 128))
    return {
        "q": n((H, D, N)).astype(np.float32),
        "qa": (np.random.uniform(0.5, 2.0, D) * s)[:, None].astype(np.float32),
        "ka": np.tile(np.random.uniform(0.5, 2.0, D) / s, (128, 1)).astype(np.float32),
        "k": n((H, N, D)).astype(np.float32),
        "t": t.reshape(N, 1).astype(np.float32),
        "v": (v / t[:, None]).astype(np.float32),
        "og": n((H, N, 128)).astype(np.float32),
    }


def reference(q, qa, ka, k, t, v, og):
    fq = (np.where(f64(q) > 0, f64(q) + 1.0, np.exp(np.minimum(f64(q), 0.0)))) * f64(qa)
    fk = (np.where(f64(k) > 0, f64(k) + 1.0, np.exp(np.minimum(f64(k), 0.0)))) * f64(t) * f64(ka)[:1]
    S = (mxq(fk, 1, "e4m3").transpose(0, 2, 1) @ mxq(f64(v), 1, "e4m3")) / N
    y = mxq(fq, 1, "e4m3").transpose(0, 2, 1) @ mxq(S, 1, "e4m3")
    y = y / (1.0 + np.exp(-f64(og)))
    return y

@@ -1,0 +1,321 @@
+from contextlib import ExitStack
+
+import concourse.mybir as mybir
+
+H, D, N = 8, 128, 512
+FLOPS = 2 * 2 * H * N * D * D
+
+F32 = mybir.dt.float32
+BF16 = mybir.dt.bfloat16
+I32 = mybir.dt.int32
+U8 = mybir.dt.uint8
+FP8X4 = mybir.dt.float8_e4m3fn_x4
+ACT = mybir.ActivationFunctionType
+ALU = mybir.AluOpType
+
+P = 128
+PACK = 4
+ROWS = 32
+SETS = H // PACK
+
+
+def tile_rows_lin_elu1_gate_kernel(tc, q, qa, ka, k, t, v, og, out):
+    nc = tc.nc
+    with ExitStack() as ctx:
+        keep = ctx.enter_context(tc.tile_pool(name="keep", bufs=1))
+        work = ctx.enter_context(tc.tile_pool(name="work", bufs=4))
+        psum = ctx.enter_context(tc.psum_pool(name="psum", bufs=1))
+        ctx.enter_context(tc.manual_schedule())
+
+        def kept(name, count, shape, dtype):
+            return [keep.tile(shape, dtype, name=name + str(i), align_bytes=64) for i in range(count)]
+
+        k_raw = kept("k_raw", H, [P, PACK, D], F32)
+        v_raw = kept("v_raw", H, [P, PACK, D], F32)
+        q_raw = kept("q_raw", SETS, [P, PACK * P, PACK], F32)
+        og_raw = kept("og_raw", SETS, [P, PACK, N], F32)
+        gate = kept("gate", H, [P, N], F32)
+        res = kept("res", H, [P, N], F32)
+        k_bf = kept("k_bf", SETS, [P, PACK, PACK, ROWS, PACK], BF16)
+        v_bf = kept("v_bf", SETS, [P, PACK, D, PACK], BF16)
+        q_bf = kept("q_bf", SETS, [P, PACK, P, PACK], BF16)
+        s_bf = kept("s_bf", SETS, [P, D, PACK], BF16)
+        k_codes = kept("k_codes", SETS, [P, N], I32)
+        v_codes = kept("v_codes", SETS, [P, N], I32)
+        q_codes = kept("q_codes", SETS, [P, N], I32)
+        s_codes = kept("s_codes", SETS, [P, D], I32)
+        k_scales = kept("k_scales", SETS, [P, N], U8)
+        v_scales = kept("v_scales", SETS, [P, N], U8)
+        q_scales = kept("q_scales", SETS, [P, N], U8)
+        s_scales = kept("s_scales", SETS, [P, D], U8)
+        spread = keep.tile([P, PACK, N + ROWS], I32, align_bytes=64)
+        t_sb = keep.tile([P, PACK], F32)
+        ka_sb = keep.tile([P, D], F32)
+        qa_sb = keep.tile([P, PACK], F32)
+        tka = keep.tile([P, PACK, D], F32)
+        warm = keep.tile([P, 2], F32)
+        state_ps = [psum.tile([P, PACK, D], F32, name="state_ps" + str(i)) for i in range(SETS)]
+        y_ps = [psum.tile([P, PACK, D], F32, name="y_ps" + str(i)) for i in range(PACK)]
+
+        def load_k(h):
+            nc.sync.dma_start(out=k_raw[h][:], in_=k[h].rearrange("(p j) d -> p j d", j=PACK))
+
+        def load_v(h):
+            nc.sync.dma_start(out=v_raw[h][:], in_=v[h].rearrange("(p j) d -> p j d", j=PACK))
+
+        def load_q(a):
+            nc.sync.dma_start(
+                out=q_raw[a][:].rearrange("p x r -> p (x r)"),
+                in_=q[PACK * a : PACK * (a + 1)].rearrange("c (p j) n -> (c p) (j n)", j=PACK),
+            )
+
+        def load_og(a):
+            nc.sync.dma_start(
+                out=og_raw[a][:], in_=og[PACK * a : PACK * (a + 1)].rearrange("c (s r) e -> s c (r e)", r=PACK)
+            )
+
+        nc.scalar.dma_start(out=t_sb[:], in_=t.rearrange("(p j) o -> p (j o)", j=PACK))
+        nc.scalar.dma_start(out=ka_sb[:], in_=ka)
+        for h in range(H):
+            load_k(h)
+        load_v(0)
+        load_v(1)
+        load_q(0)
+        for c in range(PACK):
+            nc.sync.dma_start(out=qa_sb[ROWS * c : ROWS * (c + 1), :], in_=qa.rearrange("(p j) o -> p (j o)", j=PACK))
+        for h in range(2, 6):
+            load_v(h)
+        load_q(1)
+        load_v(6)
+        load_v(7)
+        load_og(0)
+        load_og(1)
+
+        nc.vector.memset(warm[:, 0:1], 0.0)
+        nc.scalar.activation(out=warm[:, 1:2], in_=warm[:, 0:1], func=ACT.Exp)
+        nc.gpsimd.memset(spread[:], 0)
+
+        def low_part(x, shape, tag, on_vector):
+            low = work.tile(shape, F32, name="low_" + tag)
+            if on_vector:
+                nc.vector.tensor_scalar(out=low[:], in0=x, scalar1=0.0, scalar2=None, op0=ALU.min)
+                return low, 1.0
+            nc.scalar.activation(out=low[:], in_=x, func=ACT.Relu, scale=-1.0)
+            return low, -1.0
+
+        def exp_part(low, shape, tag):
+            e = work.tile(shape, F32, name="e_" + tag)
+            nc.scalar.activation(out=e[:], in_=low[0][:], func=ACT.Exp, scale=low[1])
+            return e
+
+        def feature_map(x, e, shape, tag):
+            phi = work.tile(shape, F32, name="phi_" + tag)
+            nc.vector.scalar_tensor_tensor(out=phi[:], in0=x, scalar=0.0, in1=e[:], op0=ALU.max, op1=ALU.add)
+            return phi
+
+        def quantize(codes, scales, src):
+            nc.vector.quantize_mx(out=codes.bitcast(FP8X4), scales=scales, in_=src)
+
+        k_l, k_e, k_phi, q_l, q_e, q_phi = {}, {}, {}, {}, {}, {}
+        K_SHAPE = [P, N]
+        Q_SHAPE = [P, PACK * P, 2]
+
+        def k_low(h, on_vector=False):
+            k_l[h] = low_part(k_raw[h][:].rearrange("p j d -> p (j d)"), K_SHAPE, "k", on_vector)
+
+        def k_exp2(h):
+            k_e[h] = exp_part(k_l[h], K_SHAPE, "k")
+
+        def weights():
+            nc.vector.tensor_tensor(
+                out=tka[:],
+                in0=ka_sb[:].unsqueeze(1).to_broadcast([P, PACK, D]),
+                in1=t_sb[:].unsqueeze(2).to_broadcast([P, PACK, D]),
+                op=ALU.mult,
+            )
+
+        def k_map(h):
+            k_phi[h] = feature_map(k_raw[h][:].rearrange("p j d -> p (j d)"), k_e[h], K_SHAPE, "k")
+
+        def k_weigh(h):
+            a, c = divmod(h, PACK)
+            nc.vector.tensor_tensor(
+                out=k_bf[a][:, :, c, :, :].rearrange("p x f j -> p f j x"),
+                in0=k_phi[h][:].rearrange("p (j f x) -> p f j x", j=PACK, x=PACK),
+                in1=tka[:].rearrange("p j (f x) -> p f j x", x=PACK),
+                op=ALU.mult,
+            )
+
+        def v_round(h, on_vector=False):
+            a, c = divmod(h, PACK)
+            dst = v_bf[a][:, c, :, :].rearrange("p (g i) j -> p g j i", i=PACK)
+            src = v_raw[h][:].rearrange("p j (g i) -> p g j i", i=PACK)
+            if on_vector:
+                nc.vector.tensor_copy(out=dst, in_=src)
+            else:
+                nc.scalar.copy(out=dst, in_=src)
+
+        def k_quant(a):
+            quantize(k_codes[a][:], k_scales[a][:], k_bf[a][:].rearrange("p x c f j -> p (x c f j)"))
+
+        def v_quant(a):
+            quantize(v_codes[a][:], v_scales[a][:], v_bf[a][:].rearrange("p c e j -> p (c e j)"))
+
+        def k_move(a):
+            nc.vector.tensor_copy(
+                out=spread[:, :, 0:N].rearrange("p c (x w) -> p c x w", x=PACK)[:, :, :, 0:ROWS],
+                in_=k_codes[a][:].rearrange("p (x c f) -> p c x f", x=PACK, c=PACK),
+            )
+
+        def state(a):
+            flat = spread[:].rearrange("p c w -> p (c w)")
+            for x in range(PACK):
+                for c in range(PACK):
+                    w0 = N * c + D * x
+                    nc.tensor.matmul_mx(
+                        out=state_ps[a][:, x, :],
+                        lhsT=flat[:, w0 : w0 + D].bitcast(FP8X4),
+                        lhsT_scale=k_scales[a][:, D * x : D * (x + 1)],
+                        rhs=v_codes[a][:, D * c : D * (c + 1)].bitcast(FP8X4),
+                        rhs_scale=v_scales[a][:, D * c : D * (c + 1)],
+                        start=(c == 0),
+                        stop=(c == PACK - 1),
+                    )
+
+        def s_round(a):
+            nc.scalar.activation(
+                out=s_bf[a][:], in_=state_ps[a][:].rearrange("p x e -> p e x"), func=ACT.Copy, scale=0.5 / N
+            )
+
+        def s_quant(a):
+            quantize(s_codes[a][:], s_scales[a][:], s_bf[a][:].rearrange("p e x -> p (e x)"))
+
+        def q_low(i, on_vector=False):
+            a, u = divmod(i, 2)
+            q_l[i] = low_part(q_raw[a][:, :, 2 * u : 2 * u + 2], Q_SHAPE, "q", on_vector)
+
+        def q_exp2(i):
+            q_e[i] = exp_part(q_l[i], Q_SHAPE, "q")
+
+        def q_map(i):
+            a, u = divmod(i, 2)
+            q_phi[i] = feature_map(q_raw[a][:, :, 2 * u : 2 * u + 2], q_e[i], Q_SHAPE, "q")
+
+        def q_weigh(i):
+            a, u = divmod(i, 2)
+            nc.vector.tensor_tensor(
+                out=q_bf[a][:, 2 * u : 2 * u + 2, :, :].rearrange("p r s j -> p s j r"),
+                in0=q_phi[i][:].rearrange("p (j s) r -> p s j r", j=PACK),
+                in1=qa_sb[:].unsqueeze(1).unsqueeze(3).to_broadcast([P, P, PACK, 2]),
+                op=ALU.mult,
+            )
+
+        def q_quant(i):
+            a, u = divmod(i, 2)
+            cols = slice(2 * P * u, 2 * P * (u + 1))
+            quantize(
+                q_codes[a][:, cols],
+                q_scales[a][:, cols],
+                q_bf[a][:, 2 * u : 2 * u + 2, :, :].rearrange("p r s j -> p (r s j)"),
+            )
+
+        def read_state(h, rs):
+            a, c = divmod(h, PACK)
+            rows = slice(ROWS * c, ROWS * (c + 1))
+            for r in rs:
+                nc.tensor.matmul_mx(
+                    out=y_ps[c][:, r, :],
+                    lhsT=q_codes[a][rows, P * r : P * (r + 1)].bitcast(FP8X4),
+                    lhsT_scale=q_scales[a][rows, P * r : P * (r + 1)],
+                    rhs=s_codes[a][rows, :].bitcast(FP8X4),
+                    rhs_scale=s_scales[a][rows, :],
+                    start=True,
+                    stop=True,
+                )
+
+        def gate_tanh(h):
+            a, c = divmod(h, PACK)
+            nc.scalar.activation(out=gate[h][:], in_=og_raw[a][:, c, :], func=ACT.Tanh, scale=0.5)
+
+        def finish(h):
+            nc.vector.scalar_tensor_tensor(
+                out=res[h][:],
+                in0=gate[h][:],
+                scalar=1.0,
+                in1=y_ps[h % PACK][:].rearrange("p r e -> p (r e)"),
+                op0=ALU.add,
+                op1=ALU.mult,
+            )
+            nc.sync.dma_start(out=out[h].rearrange("(s r) e -> s (r e)", r=PACK), in_=res[h][:])
+
+        k_low(0, True)
+        k_exp2(0)
+        weights()
+        k_low(1, True)
+        k_exp2(1)
+        k_low(2, True)
+        k_map(0)
+        for h in range(1, H):
+            if h + 2 < H:
+                k_low(h + 2)
+            else:
+                v_round(h - 6)
+            if h + 1 < H:
+                k_exp2(h + 1)
+            else:
+                q_low(0)
+            k_map(h)
+            k_weigh(h - 1)
+            if h == 5:
+                k_quant(0)
+            if h == 6:
+                k_move(0)
+        v_round(2)
+        q_exp2(0)
+        v_round(3)
+        q_low(1)
+        v_round(4)
+        q_exp2(1)
+        k_weigh(H - 1)
+        q_map(0)
+        k_quant(1)
+        q_weigh(0)
+        v_quant(0)
+        state(0)
+        q_low(2)
+        v_round(5)
+        q_exp2(2)
+        q_map(1)
+        q_quant(0)
+        q_weigh(1)
+        v_round(6)
+        v_round(7)
+        q_low(3)
+        s_round(0)
+        q_exp2(3)
+        k_move(1)
+        q_map(2)
+        q_quant(1)
+        v_quant(1)
+        state(1)
+        q_weigh(2)
+        s_quant(0)
+        for c in range(PACK):
+            read_state(c, range(PACK))
+        q_map(3)
+        q_quant(2)
+        q_weigh(3)
+        gate_tanh(0)
+        s_round(1)
+        finish(0)
+        q_quant(3)
+        gate_tanh(1)
+        finish(1)
+        s_quant(1)
+        read_state(4, range(PACK))
+        read_state(5, range(PACK))
+        for h in range(2, H):
+            gate_tanh(h)
+            finish(h)
+            if h < PACK:
+                read_state(h + PACK, range(PACK))

@@ -54,8 +54,9 @@ def tile_rows_lin_elu1_gate_kernel(tc, q, qa, ka, k, t, v, og, out):
         qa_sb = keep.tile([P, PACK], F32)
         tka = keep.tile([P, PACK, D], F32)
         warm = keep.tile([P, 2], F32)
-        state_ps = [psum.tile([P, PACK, D], F32, name="state_ps" + str(i)) for i in range(SETS)]
-        y_ps = [psum.tile([P, PACK, D], F32, name="y_ps" + str(i)) for i in range(PACK)]
+        state_ps = psum.tile([P, PACK, D], F32)
+        y_ps = [psum.tile([P, PACK, D], F32, name="y_ps" + str(i)) for i in range(H - 1)]
+        y_ps.append(y_ps[PACK - 1])
 
         def load_k(h):
             nc.sync.dma_start(out=k_raw[h][:], in_=k[h].rearrange("(p j) d -> p j d", j=PACK))
@@ -76,24 +77,26 @@ def tile_rows_lin_elu1_gate_kernel(tc, q, qa, ka, k, t, v, og, out):
 
         nc.scalar.dma_start(out=t_sb[:], in_=t.rearrange("(p j) o -> p (j o)", j=PACK))
         nc.scalar.dma_start(out=ka_sb[:], in_=ka)
-        for h in range(H):
+        for h in range(H - 1):
             load_k(h)
         load_v(0)
+        load_k(H - 1)
         load_v(1)
+        load_v(2)
         load_q(0)
+        load_v(3)
         for c in range(PACK):
             nc.sync.dma_start(out=qa_sb[ROWS * c : ROWS * (c + 1), :], in_=qa.rearrange("(p j) o -> p (j o)", j=PACK))
-        for h in range(2, 6):
+        for h in range(4, 7):
             load_v(h)
         load_q(1)
-        load_v(6)
         load_v(7)
         load_og(0)
         load_og(1)
 
         nc.vector.memset(warm[:, 0:1], 0.0)
         nc.scalar.activation(out=warm[:, 1:2], in_=warm[:, 0:1], func=ACT.Exp)
-        nc.gpsimd.memset(spread[:], 0)
+        nc.vector.memset(spread[:], 0)
 
         def low_part(x, shape, tag, on_vector):
             low = work.tile(shape, F32, name="low_" + tag)
@@ -139,17 +142,19 @@ def tile_rows_lin_elu1_gate_kernel(tc, q, qa, ka, k, t, v, og, out):
 
         def k_weigh(h):
             a, c = divmod(h, PACK)
-            nc.vector.tensor_tensor(
-                out=k_bf[a][:, :, c, :, :].rearrange("p x f j -> p f j x"),
-                in0=k_phi[h][:].rearrange("p (j f x) -> p f j x", j=PACK, x=PACK),
-                in1=tka[:].rearrange("p j (f x) -> p f j x", x=PACK),
-                op=ALU.mult,
-            )
+            for u in range(2):
+                xs = slice(2 * u, 2 * u + 2)
+                nc.vector.tensor_tensor(
+                    out=k_bf[a][:, xs, c, :, :].rearrange("p x f j -> p f j x"),
+                    in0=k_phi[h][:].rearrange("p (j f x) -> p f j x", j=PACK, x=PACK)[:, :, :, xs],
+                    in1=tka[:].rearrange("p j (f x) -> p f j x", x=PACK)[:, :, :, xs],
+                    op=ALU.mult,
+                )
 
         def v_round(h, on_vector=False):
             a, c = divmod(h, PACK)
-            dst = v_bf[a][:, c, :, :].rearrange("p (g i) j -> p g j i", i=PACK)
-            src = v_raw[h][:].rearrange("p j (g i) -> p g j i", i=PACK)
+            dst = v_bf[a][:, c, :, :].rearrange("p (g i) j -> p g j i", i=2)
+            src = v_raw[h][:].rearrange("p j (g i) -> p g j i", i=2)
             if on_vector:
                 nc.vector.tensor_copy(out=dst, in_=src)
             else:
@@ -173,7 +178,7 @@ def tile_rows_lin_elu1_gate_kernel(tc, q, qa, ka, k, t, v, og, out):
                 for c in range(PACK):
                     w0 = N * c + D * x
                     nc.tensor.matmul_mx(
-                        out=state_ps[a][:, x, :],
+                        out=state_ps[:, x, :],
                         lhsT=flat[:, w0 : w0 + D].bitcast(FP8X4),
                         lhsT_scale=k_scales[a][:, D * x : D * (x + 1)],
                         rhs=v_codes[a][:, D * c : D * (c + 1)].bitcast(FP8X4),
@@ -184,7 +189,7 @@ def tile_rows_lin_elu1_gate_kernel(tc, q, qa, ka, k, t, v, og, out):
 
         def s_round(a):
             nc.scalar.activation(
-                out=s_bf[a][:], in_=state_ps[a][:].rearrange("p x e -> p e x"), func=ACT.Copy, scale=0.5 / N
+                out=s_bf[a][:], in_=state_ps[:].rearrange("p x e -> p e x"), func=ACT.Copy, scale=0.5 / N
             )
 
         def s_quant(a):
@@ -219,47 +224,51 @@ def tile_rows_lin_elu1_gate_kernel(tc, q, qa, ka, k, t, v, og, out):
                 q_bf[a][:, 2 * u : 2 * u + 2, :, :].rearrange("p r s j -> p (r s j)"),
             )
 
-        def read_state(h, rs):
-            a, c = divmod(h, PACK)
-            rows = slice(ROWS * c, ROWS * (c + 1))
+        def read_state(heads, rs):
             for r in rs:
-                nc.tensor.matmul_mx(
-                    out=y_ps[c][:, r, :],
-                    lhsT=q_codes[a][rows, P * r : P * (r + 1)].bitcast(FP8X4),
-                    lhsT_scale=q_scales[a][rows, P * r : P * (r + 1)],
-                    rhs=s_codes[a][rows, :].bitcast(FP8X4),
-                    rhs_scale=s_scales[a][rows, :],
-                    start=True,
-                    stop=True,
-                )
+                for h in heads:
+                    a, c = divmod(h, PACK)
+                    rows = slice(ROWS * c, ROWS * (c + 1))
+                    nc.tensor.matmul_mx(
+                        out=y_ps[h][:, r, :],
+                        lhsT=q_codes[a][rows, P * r : P * (r + 1)].bitcast(FP8X4),
+                        lhsT_scale=q_scales[a][rows, P * r : P * (r + 1)],
+                        rhs=s_codes[a][rows, :].bitcast(FP8X4),
+                        rhs_scale=s_scales[a][rows, :],
+                        start=True,
+                        stop=True,
+                    )
 
         def gate_tanh(h):
             a, c = divmod(h, PACK)
             nc.scalar.activation(out=gate[h][:], in_=og_raw[a][:, c, :], func=ACT.Tanh, scale=0.5)
 
-        def finish(h):
-            nc.vector.scalar_tensor_tensor(
-                out=res[h][:],
-                in0=gate[h][:],
-                scalar=1.0,
-                in1=y_ps[h % PACK][:].rearrange("p r e -> p (r e)"),
-                op0=ALU.add,
-                op1=ALU.mult,
-            )
-            nc.sync.dma_start(out=out[h].rearrange("(s r) e -> s (r e)", r=PACK), in_=res[h][:])
+        def finish(h, parts=1):
+            rows = PACK // parts
+            for i in range(parts):
+                cols = slice(i * rows * D, (i + 1) * rows * D)
+                nc.vector.scalar_tensor_tensor(
+                    out=res[h][:, cols],
+                    in0=gate[h][:, cols],
+                    scalar=1.0,
+                    in1=y_ps[h][:].rearrange("p r e -> p (r e)")[:, cols],
+                    op0=ALU.add,
+                    op1=ALU.mult,
+                )
+                nc.sync.dma_start(out=out[h].rearrange("(s r) e -> s (r e)", r=PACK)[:, cols], in_=res[h][:, cols])
 
+        weights()
         k_low(0, True)
         k_exp2(0)
-        weights()
         k_low(1, True)
         k_exp2(1)
         k_low(2, True)
         k_map(0)
         for h in range(1, H):
             if h + 2 < H:
-                k_low(h + 2)
-            else:
-                v_round(h - 6)
+                k_low(h + 2, h == 2)
+            if h >= 5:
+                v_round(h - 5)
             if h + 1 < H:
                 k_exp2(h + 1)
             else:
@@ -270,52 +279,52 @@ def tile_rows_lin_elu1_gate_kernel(tc, q, qa, ka, k, t, v, og, out):
                 k_quant(0)
             if h == 6:
                 k_move(0)
-        v_round(2)
-        q_exp2(0)
         v_round(3)
+        q_exp2(0)
+        k_weigh(H - 1)
+        v_quant(0)
+        state(0)
         q_low(1)
         v_round(4)
         q_exp2(1)
-        k_weigh(H - 1)
         q_map(0)
         k_quant(1)
         q_weigh(0)
-        v_quant(0)
-        state(0)
-        q_low(2)
         v_round(5)
+        v_round(6)
+        q_low(2)
+        s_round(0)
         q_exp2(2)
         q_map(1)
         q_quant(0)
-        q_weigh(1)
-        v_round(6)
-        v_round(7)
-        q_low(3)
-        s_round(0)
-        q_exp2(3)
         k_move(1)
+        q_weigh(1)
+        q_low(3)
+        v_round(7)
+        q_exp2(3)
+        s_quant(0)
         q_map(2)
         q_quant(1)
         v_quant(1)
+        read_state(range(4), (0, 1))
+        read_state(range(4), (2, 3))
         state(1)
         q_weigh(2)
-        s_quant(0)
-        for c in range(PACK):
-            read_state(c, range(PACK))
         q_map(3)
         q_quant(2)
         q_weigh(3)
-        gate_tanh(0)
+        for h in range(PACK):
+            gate_tanh(h)
         s_round(1)
         finish(0)
-        q_quant(3)
-        gate_tanh(1)
-        finish(1)
         s_quant(1)
-        read_state(4, range(PACK))
-        read_state(5, range(PACK))
+        q_quant(3)
+        read_state(range(4, 7), (0, 1))
+        read_state(range(4, 7), (2, 3))
+        finish(1)
         for h in range(2, H):
-            gate_tanh(h)
-            finish(h)
-            if h < PACK:
-                read_state(h + PACK, range(PACK))
+            if h >= PACK:
+                gate_tanh(h)
+            finish(h, 2 if h == H - 1 else 1)
+            if h == 3:
+                read_state((7,), range(4))

@@ -23,19 +23,19 @@ def tile_rows_lin_elu1_gate_kernel(tc, q, qa, ka, k, t, v, og, out):
     nc = tc.nc
     with ExitStack() as ctx:
         keep = ctx.enter_context(tc.tile_pool(name="keep", bufs=1))
-        work = ctx.enter_context(tc.tile_pool(name="work", bufs=4))
         psum = ctx.enter_context(tc.psum_pool(name="psum", bufs=1))
         ctx.enter_context(tc.manual_schedule())
 
         def kept(name, count, shape, dtype):
             return [keep.tile(shape, dtype, name=name + str(i), align_bytes=64) for i in range(count)]
 
-        k_raw = kept("k_raw", H, [P, PACK, D], F32)
+        k_raw = kept("k_raw", H, [P, N], F32)
         v_raw = kept("v_raw", H, [P, PACK, D], F32)
         q_raw = kept("q_raw", SETS, [P, PACK * P, PACK], F32)
         og_raw = kept("og_raw", SETS, [P, PACK, N], F32)
-        gate = kept("gate", H, [P, N], F32)
-        res = kept("res", H, [P, N], F32)
+        k_work = kept("k_work", H, [P, N], F32)
+        q_work = kept("q_work", 2 * SETS, [P, 2 * N], F32)
+        q_lin = kept("q_lin", 2, [P, PACK, 2, P], F32)
         k_bf = kept("k_bf", SETS, [P, PACK, PACK, ROWS, PACK], BF16)
         v_bf = kept("v_bf", SETS, [P, PACK, D, PACK], BF16)
         q_bf = kept("q_bf", SETS, [P, PACK, P, PACK], BF16)
@@ -58,8 +58,8 @@ def tile_rows_lin_elu1_gate_kernel(tc, q, qa, ka, k, t, v, og, out):
         y_ps = [psum.tile([P, PACK, D], F32, name="y_ps" + str(i)) for i in range(H - 1)]
         y_ps.append(y_ps[PACK - 1])
 
-        def load_k(h):
-            nc.sync.dma_start(out=k_raw[h][:], in_=k[h].rearrange("(p j) d -> p j d", j=PACK))
+        def load_k(h, cols=slice(0, N)):
+            nc.sync.dma_start(out=k_raw[h][:, cols], in_=k[h].rearrange("(p j) d -> p (j d)", j=PACK)[:, cols])
 
         def load_v(h):
             nc.sync.dma_start(out=v_raw[h][:], in_=v[h].rearrange("(p j) d -> p j d", j=PACK))
@@ -77,18 +77,25 @@ def tile_rows_lin_elu1_gate_kernel(tc, q, qa, ka, k, t, v, og, out):
 
         nc.scalar.dma_start(out=t_sb[:], in_=t.rearrange("(p j) o -> p (j o)", j=PACK))
         nc.scalar.dma_start(out=ka_sb[:], in_=ka)
-        for h in range(H - 1):
-            load_k(h)
+        load_k(0, cols=slice(0, N // 2))
+        load_k(0, cols=slice(N // 2, N))
+        load_k(1)
+        load_k(2)
+        load_k(3)
         load_v(0)
-        load_k(H - 1)
+        load_k(4)
+        load_k(5)
+        load_k(6)
         load_v(1)
         load_v(2)
-        load_q(0)
+        load_k(7)
         load_v(3)
+        load_v(4)
+        load_q(0)
         for c in range(PACK):
             nc.sync.dma_start(out=qa_sb[ROWS * c : ROWS * (c + 1), :], in_=qa.rearrange("(p j) o -> p (j o)", j=PACK))
-        for h in range(4, 7):
-            load_v(h)
+        load_v(5)
+        load_v(6)
         load_q(1)
         load_v(7)
         load_og(0)
@@ -98,36 +105,25 @@ def tile_rows_lin_elu1_gate_kernel(tc, q, qa, ka, k, t, v, og, out):
         nc.scalar.activation(out=warm[:, 1:2], in_=warm[:, 0:1], func=ACT.Exp)
         nc.vector.memset(spread[:], 0)
 
-        def low_part(x, shape, tag, on_vector):
-            low = work.tile(shape, F32, name="low_" + tag)
+        def low_part(low, x, on_vector):
             if on_vector:
-                nc.vector.tensor_scalar(out=low[:], in0=x, scalar1=0.0, scalar2=None, op0=ALU.min)
-                return low, 1.0
-            nc.scalar.activation(out=low[:], in_=x, func=ACT.Relu, scale=-1.0)
-            return low, -1.0
-
-        def exp_part(low, shape, tag):
-            e = work.tile(shape, F32, name="e_" + tag)
-            nc.scalar.activation(out=e[:], in_=low[0][:], func=ACT.Exp, scale=low[1])
-            return e
-
-        def feature_map(x, e, shape, tag):
-            phi = work.tile(shape, F32, name="phi_" + tag)
-            nc.vector.scalar_tensor_tensor(out=phi[:], in0=x, scalar=0.0, in1=e[:], op0=ALU.max, op1=ALU.add)
-            return phi
+                nc.vector.tensor_scalar(out=low, in0=x, scalar1=0.0, scalar2=None, op0=ALU.min)
+                return 1.0
+            nc.scalar.activation(out=low, in_=x, func=ACT.Relu, scale=-1.0)
+            return -1.0
 
         def quantize(codes, scales, src):
             nc.vector.quantize_mx(out=codes.bitcast(FP8X4), scales=scales, in_=src)
 
-        k_l, k_e, k_phi, q_l, q_e, q_phi = {}, {}, {}, {}, {}, {}
-        K_SHAPE = [P, N]
-        Q_SHAPE = [P, PACK * P, 2]
+        sign = {}
 
-        def k_low(h, on_vector=False):
-            k_l[h] = low_part(k_raw[h][:].rearrange("p j d -> p (j d)"), K_SHAPE, "k", on_vector)
+        def k_low(h, on_vector=False, cols=slice(0, N)):
+            sign["k", h, cols.start] = low_part(k_work[h][:, cols], k_raw[h][:, cols], on_vector)
 
-        def k_exp2(h):
-            k_e[h] = exp_part(k_l[h], K_SHAPE, "k")
+        def k_exp(h, cols=slice(0, N)):
+            nc.scalar.activation(
+                out=k_work[h][:, cols], in_=k_work[h][:, cols], func=ACT.Exp, scale=sign["k", h, cols.start]
+            )
 
         def weights():
             nc.vector.tensor_tensor(
@@ -137,19 +133,24 @@ def tile_rows_lin_elu1_gate_kernel(tc, q, qa, ka, k, t, v, og, out):
                 op=ALU.mult,
             )
 
-        def k_map(h):
-            k_phi[h] = feature_map(k_raw[h][:].rearrange("p j d -> p (j d)"), k_e[h], K_SHAPE, "k")
+        def k_map(h, cols=slice(0, N)):
+            nc.vector.scalar_tensor_tensor(
+                out=k_work[h][:, cols],
+                in0=k_raw[h][:, cols],
+                scalar=0.0,
+                in1=k_work[h][:, cols],
+                op0=ALU.max,
+                op1=ALU.add,
+            )
 
         def k_weigh(h):
             a, c = divmod(h, PACK)
-            for u in range(2):
-                xs = slice(2 * u, 2 * u + 2)
-                nc.vector.tensor_tensor(
-                    out=k_bf[a][:, xs, c, :, :].rearrange("p x f j -> p f j x"),
-                    in0=k_phi[h][:].rearrange("p (j f x) -> p f j x", j=PACK, x=PACK)[:, :, :, xs],
-                    in1=tka[:].rearrange("p j (f x) -> p f j x", x=PACK)[:, :, :, xs],
-                    op=ALU.mult,
-                )
+            nc.vector.tensor_tensor(
+                out=k_bf[a][:, :, c, :, :].rearrange("p x f j -> p f j x"),
+                in0=k_work[h][:].rearrange("p (j f x) -> p f j x", j=PACK, x=PACK),
+                in1=tka[:].rearrange("p j (f x) -> p f j x", x=PACK),
+                op=ALU.mult,
+            )
 
         def v_round(h, on_vector=False):
             a, c = divmod(h, PACK)
@@ -195,25 +196,57 @@ def tile_rows_lin_elu1_gate_kernel(tc, q, qa, ka, k, t, v, og, out):
         def s_quant(a):
             quantize(s_codes[a][:], s_scales[a][:], s_bf[a][:].rearrange("p e x -> p (e x)"))
 
-        def q_low(i, on_vector=False):
+        def q_half(i):
             a, u = divmod(i, 2)
-            q_l[i] = low_part(q_raw[a][:, :, 2 * u : 2 * u + 2], Q_SHAPE, "q", on_vector)
+            return q_raw[a][:, :, 2 * u : 2 * u + 2]
 
-        def q_exp2(i):
-            q_e[i] = exp_part(q_l[i], Q_SHAPE, "q")
+        def q_low(i, on_vector=False):
+            if i < 2:
+                low, x = q_work[i][:].rearrange("p (y r) -> p y r", r=2), q_half(i)
+            else:
+                low = q_work[i][:].rearrange("p (j r s) -> p j s r", j=PACK, r=2)
+                x = q_half(i).rearrange("p (j s) r -> p j s r", j=PACK)
+            sign["q", i] = low_part(low, x, on_vector)
+
+        def q_exp(i):
+            nc.scalar.activation(out=q_work[i][:], in_=q_work[i][:], func=ACT.Exp, scale=sign["q", i])
 
         def q_map(i):
-            a, u = divmod(i, 2)
-            q_phi[i] = feature_map(q_raw[a][:, :, 2 * u : 2 * u + 2], q_e[i], Q_SHAPE, "q")
+            if i < 2:
+                e = q_work[i][:].rearrange("p (y r) -> p y r", r=2)
+                nc.vector.scalar_tensor_tensor(out=e, in0=q_half(i), scalar=0.0, in1=e, op0=ALU.max, op1=ALU.add)
+            else:
+                nc.vector.tensor_scalar(
+                    out=q_lin[i - 2][:].rearrange("p j r s -> p j s r"),
+                    in0=q_half(i).rearrange("p (j s) r -> p j s r", j=PACK),
+                    scalar1=0.0,
+                    scalar2=1.0,
+                    op0=ALU.max,
+                    op1=ALU.add,
+                )
+
+        def q_scale(i):
+            for j in range(PACK):
+                lin = q_lin[i - 2][:, j, :, :].rearrange("p r s -> p (r s)")
+                nc.scalar.activation(out=lin, in_=lin, func=ACT.Copy, scale=qa_sb[:, j : j + 1])
 
         def q_weigh(i):
             a, u = divmod(i, 2)
-            nc.vector.tensor_tensor(
-                out=q_bf[a][:, 2 * u : 2 * u + 2, :, :].rearrange("p r s j -> p s j r"),
-                in0=q_phi[i][:].rearrange("p (j s) r -> p s j r", j=PACK),
-                in1=qa_sb[:].unsqueeze(1).unsqueeze(3).to_broadcast([P, P, PACK, 2]),
-                op=ALU.mult,
-            )
+            dst = q_bf[a][:, 2 * u : 2 * u + 2, :, :]
+            if i < 2:
+                nc.vector.tensor_tensor(
+                    out=dst.rearrange("p r s j -> p s j r"),
+                    in0=q_work[i][:].rearrange("p (j s r) -> p s j r", j=PACK, r=2),
+                    in1=qa_sb[:].unsqueeze(1).unsqueeze(3).to_broadcast([P, P, PACK, 2]),
+                    op=ALU.mult,
+                )
+            else:
+                nc.vector.tensor_tensor(
+                    out=dst.rearrange("p r s j -> p (r s) j").rearrange("p (g w) j -> p g j w", w=2),
+                    in0=q_work[i][:].rearrange("p (j g w) -> p g j w", j=PACK, w=2),
+                    in1=q_lin[i - 2][:].rearrange("p j r s -> p j (r s)").rearrange("p j (g w) -> p g j w", w=2),
+                    op=ALU.mult,
+                )
 
         def q_quant(i):
             a, u = divmod(i, 2)
@@ -241,90 +274,119 @@ def tile_rows_lin_elu1_gate_kernel(tc, q, qa, ka, k, t, v, og, out):
 
         def gate_tanh(h):
             a, c = divmod(h, PACK)
-            nc.scalar.activation(out=gate[h][:], in_=og_raw[a][:, c, :], func=ACT.Tanh, scale=0.5)
+            nc.scalar.activation(out=og_raw[a][:, c, :], in_=og_raw[a][:, c, :], func=ACT.Tanh, scale=0.5)
 
         def finish(h, parts=1):
             rows = PACK // parts
+            gate = og_raw[h // PACK][:, h % PACK, :]
             for i in range(parts):
                 cols = slice(i * rows * D, (i + 1) * rows * D)
                 nc.vector.scalar_tensor_tensor(
-                    out=res[h][:, cols],
-                    in0=gate[h][:, cols],
+                    out=gate[:, cols],
+                    in0=gate[:, cols],
                     scalar=1.0,
                     in1=y_ps[h][:].rearrange("p r e -> p (r e)")[:, cols],
                     op0=ALU.add,
                     op1=ALU.mult,
                 )
-                nc.sync.dma_start(out=out[h].rearrange("(s r) e -> s (r e)", r=PACK)[:, cols], in_=res[h][:, cols])
+                nc.sync.dma_start(out=out[h].rearrange("(s r) e -> s (r e)", r=PACK)[:, cols], in_=gate[:, cols])
 
+        k_low(0, cols=slice(0, N // 2))
+        k_exp(0, cols=slice(0, N // 2))
         weights()
-        k_low(0, True)
-        k_exp2(0)
-        k_low(1, True)
-        k_exp2(1)
+        k_low(0, True, cols=slice(N // 2, N))
+        k_exp(0, cols=slice(N // 2, N))
+        k_low(1)
+        k_map(0, cols=slice(0, N // 2))
+        k_exp(1)
+        k_map(0, cols=slice(N // 2, N))
         k_low(2, True)
-        k_map(0)
-        for h in range(1, H):
-            if h + 2 < H:
-                k_low(h + 2, h == 2)
-            if h >= 5:
-                v_round(h - 5)
-            if h + 1 < H:
-                k_exp2(h + 1)
-            else:
-                q_low(0)
-            k_map(h)
-            k_weigh(h - 1)
-            if h == 5:
-                k_quant(0)
-            if h == 6:
-                k_move(0)
+        k_weigh(0)
+        k_low(3, True)
+        k_exp(2)
+        v_round(0)
+        k_exp(3)
+        k_map(1)
+        k_map(2)
+        k_low(4)
+        k_weigh(1)
+        k_low(5)
+        k_map(3)
+        k_weigh(2)
+        k_low(6, True)
+        k_weigh(3)
+        k_exp(4)
+        k_exp(5)
+        k_exp(6)
+        v_round(1)
+        k_map(4)
+        k_quant(0)
+        k_low(7)
+        k_weigh(4)
+        v_round(2)
+        k_map(5)
         v_round(3)
-        q_exp2(0)
-        k_weigh(H - 1)
-        v_quant(0)
-        state(0)
-        q_low(1)
+        k_map(6)
+        k_exp(7)
+        k_move(0)
         v_round(4)
-        q_exp2(1)
+        q_low(0)
+        k_weigh(5)
+        k_map(7)
+        v_quant(0)
+        k_weigh(6)
+        v_round(5)
+        q_exp(0)
+        q_low(1, True)
+        q_exp(1)
+        k_weigh(7)
+        v_round(6)
         q_map(0)
         k_quant(1)
-        q_weigh(0)
-        v_round(5)
-        v_round(6)
         q_low(2)
-        s_round(0)
-        q_exp2(2)
         q_map(1)
-        q_quant(0)
-        k_move(1)
-        q_weigh(1)
-        q_low(3)
         v_round(7)
-        q_exp2(3)
-        s_quant(0)
         q_map(2)
-        q_quant(1)
         v_quant(1)
+        state(0)
+        s_round(0)
+        q_exp(2)
+        k_move(1)
+        q_map(3)
+        q_weigh(0)
+        q_scale(2)
+        q_low(3)
+        q_scale(3)
+        q_exp(3)
+        q_weigh(1)
+        state(1)
+        q_quant(0)
+        s_quant(0)
+        q_weigh(2)
+        s_round(1)
+        q_quant(1)
         read_state(range(4), (0, 1))
         read_state(range(4), (2, 3))
-        state(1)
-        q_weigh(2)
-        q_map(3)
         q_quant(2)
         q_weigh(3)
-        for h in range(PACK):
-            gate_tanh(h)
-        s_round(1)
-        finish(0)
+        gate_tanh(0)
         s_quant(1)
-        q_quant(3)
+        gate_tanh(1)
         read_state(range(4, 7), (0, 1))
-        read_state(range(4, 7), (2, 3))
+        gate_tanh(2)
+        finish(0)
+        gate_tanh(3)
         finish(1)
-        for h in range(2, H):
-            if h >= PACK:
-                gate_tanh(h)
-            finish(h, 2 if h == H - 1 else 1)
-            if h == 3:
-                read_state((7,), range(4))
+        q_quant(3)
+        finish(2)
+        gate_tanh(4)
+        read_state(range(4, 7), (2, 3))
+        gate_tanh(5)
+        finish(3)
+        gate_tanh(6)
+        read_state((7,), range(4))
+        finish(4)
+        finish(5)
+        finish(6)
+        gate_tanh(7)
+        finish(7, 2)

@@ -35,7 +35,7 @@ def tile_rows_lin_elu1_gate_kernel(tc, q, qa, ka, k, t, v, og, out):
         og_raw = kept("og_raw", SETS, [P, PACK, N], F32)
         k_work = kept("k_work", H, [P, N], F32)
         q_work = kept("q_work", 2 * SETS, [P, 2 * N], F32)
-        q_lin = kept("q_lin", 2, [P, PACK, 2, P], F32)
+        q_lin = kept("q_lin", 2 * SETS, [P, PACK, 2, P], F32)
         k_bf = kept("k_bf", SETS, [P, PACK, PACK, ROWS, PACK], BF16)
         v_bf = kept("v_bf", SETS, [P, PACK, D, PACK], BF16)
         q_bf = kept("q_bf", SETS, [P, PACK, P, PACK], BF16)
@@ -82,23 +82,23 @@ def tile_rows_lin_elu1_gate_kernel(tc, q, qa, ka, k, t, v, og, out):
         load_k(1)
         load_k(2)
         load_k(3)
-        load_v(0)
         load_k(4)
         load_k(5)
         load_k(6)
-        load_v(1)
-        load_v(2)
-        load_k(7)
-        load_v(3)
-        load_v(4)
+        load_v(0)
         load_q(0)
         for c in range(PACK):
             nc.sync.dma_start(out=qa_sb[ROWS * c : ROWS * (c + 1), :], in_=qa.rearrange("(p j) o -> p (j o)", j=PACK))
+        load_v(1)
+        load_v(2)
+        load_v(3)
+        load_k(7)
+        load_q(1)
+        load_v(4)
         load_v(5)
         load_v(6)
-        load_q(1)
-        load_v(7)
         load_og(0)
+        load_v(7)
         load_og(1)
 
         nc.vector.memset(warm[:, 0:1], 0.0)
@@ -201,7 +201,7 @@ def tile_rows_lin_elu1_gate_kernel(tc, q, qa, ka, k, t, v, og, out):
             return q_raw[a][:, :, 2 * u : 2 * u + 2]
 
         def q_low(i, on_vector=False):
-            if i < 2:
+            if i < 0:
                 low, x = q_work[i][:].rearrange("p (y r) -> p y r", r=2), q_half(i)
             else:
                 low = q_work[i][:].rearrange("p (j r s) -> p j s r", j=PACK, r=2)
@@ -212,12 +212,12 @@ def tile_rows_lin_elu1_gate_kernel(tc, q, qa, ka, k, t, v, og, out):
             nc.scalar.activation(out=q_work[i][:], in_=q_work[i][:], func=ACT.Exp, scale=sign["q", i])
 
         def q_map(i):
-            if i < 2:
+            if i < 0:
                 e = q_work[i][:].rearrange("p (y r) -> p y r", r=2)
                 nc.vector.scalar_tensor_tensor(out=e, in0=q_half(i), scalar=0.0, in1=e, op0=ALU.max, op1=ALU.add)
             else:
                 nc.vector.tensor_scalar(
-                    out=q_lin[i - 2][:].rearrange("p j r s -> p j s r"),
+                    out=q_lin[i][:].rearrange("p j r s -> p j s r"),
                     in0=q_half(i).rearrange("p (j s) r -> p j s r", j=PACK),
                     scalar1=0.0,
                     scalar2=1.0,
@@ -227,13 +227,13 @@ def tile_rows_lin_elu1_gate_kernel(tc, q, qa, ka, k, t, v, og, out):
 
         def q_scale(i):
             for j in range(PACK):
-                lin = q_lin[i - 2][:, j, :, :].rearrange("p r s -> p (r s)")
+                lin = q_lin[i][:, j, :, :].rearrange("p r s -> p (r s)")
                 nc.scalar.activation(out=lin, in_=lin, func=ACT.Copy, scale=qa_sb[:, j : j + 1])
 
         def q_weigh(i):
             a, u = divmod(i, 2)
             dst = q_bf[a][:, 2 * u : 2 * u + 2, :, :]
-            if i < 2:
+            if i < 0:
                 nc.vector.tensor_tensor(
                     out=dst.rearrange("p r s j -> p s j r"),
                     in0=q_work[i][:].rearrange("p (j s r) -> p s j r", j=PACK, r=2),
@@ -244,7 +244,7 @@ def tile_rows_lin_elu1_gate_kernel(tc, q, qa, ka, k, t, v, og, out):
                 nc.vector.tensor_tensor(
                     out=dst.rearrange("p r s j -> p (r s) j").rearrange("p (g w) j -> p g j w", w=2),
                     in0=q_work[i][:].rearrange("p (j g w) -> p g j w", j=PACK, w=2),
-                    in1=q_lin[i - 2][:].rearrange("p j r s -> p j (r s)").rearrange("p j (g w) -> p g j w", w=2),
+                    in1=q_lin[i][:].rearrange("p j r s -> p j (r s)").rearrange("p j (g w) -> p g j w", w=2),
                     op=ALU.mult,
                 )
 
@@ -291,102 +291,104 @@ def tile_rows_lin_elu1_gate_kernel(tc, q, qa, ka, k, t, v, og, out):
                 )
                 nc.sync.dma_start(out=out[h].rearrange("(s r) e -> s (r e)", r=PACK)[:, cols], in_=gate[:, cols])
 
-        k_low(0, cols=slice(0, N // 2))
+        k_low(0, True, cols=slice(0, N // 2))
+        k_low(0, True, cols=slice(N // 2, N))
         k_exp(0, cols=slice(0, N // 2))
         weights()
-        k_low(0, True, cols=slice(N // 2, N))
         k_exp(0, cols=slice(N // 2, N))
         k_low(1)
         k_map(0, cols=slice(0, N // 2))
-        k_exp(1)
         k_map(0, cols=slice(N // 2, N))
+        k_exp(1)
         k_low(2, True)
         k_weigh(0)
         k_low(3, True)
         k_exp(2)
-        v_round(0)
-        k_exp(3)
         k_map(1)
         k_map(2)
         k_low(4)
+        k_exp(3)
         k_weigh(1)
-        k_low(5)
         k_map(3)
-        k_weigh(2)
-        k_low(6, True)
-        k_weigh(3)
         k_exp(4)
-        k_exp(5)
-        k_exp(6)
-        v_round(1)
+        k_weigh(2)
         k_map(4)
-        k_quant(0)
-        k_low(7)
-        k_weigh(4)
-        v_round(2)
+        k_low(5)
+        k_weigh(3)
+        k_low(6)
+        k_exp(5)
         k_map(5)
+        k_weigh(4)
+        k_quant(0)
+        q_map(0)
+        k_exp(6)
+        v_round(0)
+        q_low(0)
+        q_low(1, True)
+        v_round(1)
+        k_move(0)
+        v_round(2)
+        k_weigh(5)
+        q_scale(0)
         v_round(3)
         k_map(6)
-        k_exp(7)
-        k_move(0)
-        v_round(4)
-        q_low(0)
-        k_weigh(5)
-        k_map(7)
-        v_quant(0)
-        k_weigh(6)
-        v_round(5)
+        k_low(7, True)
         q_exp(0)
-        q_low(1, True)
-        q_exp(1)
-        k_weigh(7)
-        v_round(6)
-        q_map(0)
-        k_quant(1)
-        q_low(2)
+        v_quant(0)
+        k_exp(7)
         q_map(1)
-        v_round(7)
-        q_map(2)
-        v_quant(1)
-        state(0)
-        s_round(0)
-        q_exp(2)
-        k_move(1)
-        q_map(3)
         q_weigh(0)
-        q_scale(2)
-        q_low(3)
-        q_scale(3)
-        q_exp(3)
-        q_weigh(1)
-        state(1)
+        q_low(2, True)
+        q_map(2)
+        q_exp(1)
         q_quant(0)
+        v_round(4)
+        k_weigh(6)
+        q_scale(1)
+        k_map(7)
+        v_round(5)
+        state(0)
+        v_round(6)
+        s_round(0)
+        q_weigh(1)
+        k_weigh(7)
         s_quant(0)
-        q_weigh(2)
-        s_round(1)
-        q_quant(1)
         read_state(range(4), (0, 1))
+        q_quant(1)
+        k_quant(1)
+        v_round(7)
         read_state(range(4), (2, 3))
-        q_quant(2)
-        q_weigh(3)
+        v_quant(1)
+        k_move(1)
+        q_low(3, True)
+        q_exp(2)
         gate_tanh(0)
-        s_quant(1)
+        q_map(3)
+        state(1)
+        q_scale(2)
         gate_tanh(1)
+        q_weigh(2)
+        finish(0)
+        q_exp(3)
+        finish(1)
+        q_quant(2)
+        q_scale(3)
+        q_weigh(3)
+        s_round(1)
+        s_quant(1)
+        q_quant(3)
         read_state(range(4, 7), (0, 1))
         gate_tanh(2)
-        finish(0)
         gate_tanh(3)
-        finish(1)
-        q_quant(3)
         finish(2)
         gate_tanh(4)
-        read_state(range(4, 7), (2, 3))
         gate_tanh(5)
-        finish(3)
         gate_tanh(6)
-        read_state((7,), range(4))
+        finish(3)
+        read_state(range(4, 7), (2, 3))
         finish(4)
         finish(5)
-        finish(6)
         gate_tanh(7)
+        read_state((7,), range(4))
+        finish(6)
         finish(7, 2)

from contextlib import ExitStack

import concourse.mybir as mybir

H, D, N = 8, 128, 512
FLOPS = 2 * 2 * H * N * D * D

F32 = mybir.dt.float32
BF16 = mybir.dt.bfloat16
I32 = mybir.dt.int32
U8 = mybir.dt.uint8
FP8X4 = mybir.dt.float8_e4m3fn_x4
ACT = mybir.ActivationFunctionType
ALU = mybir.AluOpType

P = 128
PACK = 4
ROWS = 32
SETS = H // PACK


def tile_rows_lin_elu1_gate_kernel(tc, q, qa, ka, k, t, v, og, out):
    nc = tc.nc
    with ExitStack() as ctx:
        keep = ctx.enter_context(tc.tile_pool(name="keep", bufs=1))
        psum = ctx.enter_context(tc.psum_pool(name="psum", bufs=1))
        ctx.enter_context(tc.manual_schedule())

        def kept(name, count, shape, dtype):
            return [keep.tile(shape, dtype, name=name + str(i), align_bytes=64) for i in range(count)]

        k_raw = kept("k_raw", H, [P, N], F32)
        v_raw = kept("v_raw", H, [P, PACK, D], F32)
        q_raw = kept("q_raw", SETS, [P, PACK * P, PACK], F32)
        og_raw = kept("og_raw", SETS, [P, PACK, N], F32)
        k_work = kept("k_work", H, [P, N], F32)
        q_work = kept("q_work", 2 * SETS, [P, 2 * N], F32)
        q_lin = kept("q_lin", 2 * SETS, [P, PACK, 2, P], F32)
        k_bf = kept("k_bf", SETS, [P, PACK, PACK, ROWS, PACK], BF16)
        v_bf = kept("v_bf", SETS, [P, PACK, D, PACK], BF16)
        q_bf = kept("q_bf", SETS, [P, PACK, P, PACK], BF16)
        s_bf = kept("s_bf", SETS, [P, D, PACK], BF16)
        k_codes = kept("k_codes", SETS, [P, N], I32)
        v_codes = kept("v_codes", SETS, [P, N], I32)
        q_codes = kept("q_codes", SETS, [P, N], I32)
        s_codes = kept("s_codes", SETS, [P, D], I32)
        k_scales = kept("k_scales", SETS, [P, N], U8)
        v_scales = kept("v_scales", SETS, [P, N], U8)
        q_scales = kept("q_scales", SETS, [P, N], U8)
        s_scales = kept("s_scales", SETS, [P, D], U8)
        spread = keep.tile([P, PACK, N + ROWS], I32, align_bytes=64)
        t_sb = keep.tile([P, PACK], F32)
        ka_sb = keep.tile([P, D], F32)
        qa_sb = keep.tile([P, PACK], F32)
        tka = keep.tile([P, PACK, D], F32)
        warm = keep.tile([P, 2], F32)
        state_ps = psum.tile([P, PACK, D], F32)
        y_ps = [psum.tile([P, PACK, D], F32, name="y_ps" + str(i)) for i in range(H - 1)]
        y_ps.append(y_ps[PACK - 1])

        def load_k(h, cols=slice(0, N)):
            nc.sync.dma_start(out=k_raw[h][:, cols], in_=k[h].rearrange("(p j) d -> p (j d)", j=PACK)[:, cols])

        def load_v(h):
            nc.sync.dma_start(out=v_raw[h][:], in_=v[h].rearrange("(p j) d -> p j d", j=PACK))

        def load_q(a):
            nc.sync.dma_start(
                out=q_raw[a][:].rearrange("p x r -> p (x r)"),
                in_=q[PACK * a : PACK * (a + 1)].rearrange("c (p j) n -> (c p) (j n)", j=PACK),
            )

        def load_og(a):
            nc.sync.dma_start(
                out=og_raw[a][:], in_=og[PACK * a : PACK * (a + 1)].rearrange("c (s r) e -> s c (r e)", r=PACK)
            )

        nc.scalar.dma_start(out=t_sb[:], in_=t.rearrange("(p j) o -> p (j o)", j=PACK))
        nc.scalar.dma_start(out=ka_sb[:], in_=ka)
        load_k(0, cols=slice(0, N // 2))
        load_k(0, cols=slice(N // 2, N))
        load_k(1)
        load_k(2)
        load_k(3)
        load_k(4)
        load_k(5)
        load_k(6)
        load_v(0)
        load_q(0)
        for c in range(PACK):
            nc.sync.dma_start(out=qa_sb[ROWS * c : ROWS * (c + 1), :], in_=qa.rearrange("(p j) o -> p (j o)", j=PACK))
        load_v(1)
        load_v(2)
        load_v(3)
        load_k(7)
        load_q(1)
        load_v(4)
        load_v(5)
        load_v(6)
        load_og(0)
        load_v(7)
        load_og(1)

        nc.vector.memset(warm[:, 0:1], 0.0)
        nc.scalar.activation(out=warm[:, 1:2], in_=warm[:, 0:1], func=ACT.Exp)
        nc.vector.memset(spread[:], 0)

        def low_part(low, x, on_vector):
            if on_vector:
                nc.vector.tensor_scalar(out=low, in0=x, scalar1=0.0, scalar2=None, op0=ALU.min)
                return 1.0
            nc.scalar.activation(out=low, in_=x, func=ACT.Relu, scale=-1.0)
            return -1.0

        def quantize(codes, scales, src):
            nc.vector.quantize_mx(out=codes.bitcast(FP8X4), scales=scales, in_=src)

        sign = {}

        def k_low(h, on_vector=False, cols=slice(0, N)):
            sign["k", h, cols.start] = low_part(k_work[h][:, cols], k_raw[h][:, cols], on_vector)

        def k_exp(h, cols=slice(0, N)):
            nc.scalar.activation(
                out=k_work[h][:, cols], in_=k_work[h][:, cols], func=ACT.Exp, scale=sign["k", h, cols.start]
            )

        def weights():
            nc.vector.tensor_tensor(
                out=tka[:],
                in0=ka_sb[:].unsqueeze(1).to_broadcast([P, PACK, D]),
                in1=t_sb[:].unsqueeze(2).to_broadcast([P, PACK, D]),
                op=ALU.mult,
            )

        def k_map(h, cols=slice(0, N)):
            nc.vector.scalar_tensor_tensor(
                out=k_work[h][:, cols],
                in0=k_raw[h][:, cols],
                scalar=0.0,
                in1=k_work[h][:, cols],
                op0=ALU.max,
                op1=ALU.add,
            )

        def k_weigh(h):
            a, c = divmod(h, PACK)
            nc.vector.tensor_tensor(
                out=k_bf[a][:, :, c, :, :].rearrange("p x f j -> p f j x"),
                in0=k_work[h][:].rearrange("p (j f x) -> p f j x", j=PACK, x=PACK),
                in1=tka[:].rearrange("p j (f x) -> p f j x", x=PACK),
                op=ALU.mult,
            )

        def v_round(h, on_vector=False):
            a, c = divmod(h, PACK)
            dst = v_bf[a][:, c, :, :].rearrange("p (g i) j -> p g j i", i=2)
            src = v_raw[h][:].rearrange("p j (g i) -> p g j i", i=2)
            if on_vector:
                nc.vector.tensor_copy(out=dst, in_=src)
            else:
                nc.scalar.copy(out=dst, in_=src)

        def k_quant(a):
            quantize(k_codes[a][:], k_scales[a][:], k_bf[a][:].rearrange("p x c f j -> p (x c f j)"))

        def v_quant(a):
            quantize(v_codes[a][:], v_scales[a][:], v_bf[a][:].rearrange("p c e j -> p (c e j)"))

        def k_move(a):
            nc.vector.tensor_copy(
                out=spread[:, :, 0:N].rearrange("p c (x w) -> p c x w", x=PACK)[:, :, :, 0:ROWS],
                in_=k_codes[a][:].rearrange("p (x c f) -> p c x f", x=PACK, c=PACK),
            )

        def state(a):
            flat = spread[:].rearrange("p c w -> p (c w)")
            for x in range(PACK):
                for c in range(PACK):
                    w0 = N * c + D * x
                    nc.tensor.matmul_mx(
                        out=state_ps[:, x, :],
                        lhsT=flat[:, w0 : w0 + D].bitcast(FP8X4),
                        lhsT_scale=k_scales[a][:, D * x : D * (x + 1)],
                        rhs=v_codes[a][:, D * c : D * (c + 1)].bitcast(FP8X4),
                        rhs_scale=v_scales[a][:, D * c : D * (c + 1)],
                        start=(c == 0),
                        stop=(c == PACK - 1),
                    )

        def s_round(a):
            nc.scalar.activation(
                out=s_bf[a][:], in_=state_ps[:].rearrange("p x e -> p e x"), func=ACT.Copy, scale=0.5 / N
            )

        def s_quant(a):
            quantize(s_codes[a][:], s_scales[a][:], s_bf[a][:].rearrange("p e x -> p (e x)"))

        def q_half(i):
            a, u = divmod(i, 2)
            return q_raw[a][:, :, 2 * u : 2 * u + 2]

        def q_low(i, on_vector=False):
            if i < 0:
                low, x = q_work[i][:].rearrange("p (y r) -> p y r", r=2), q_half(i)
            else:
                low = q_work[i][:].rearrange("p (j r s) -> p j s r", j=PACK, r=2)
                x = q_half(i).rearrange("p (j s) r -> p j s r", j=PACK)
            sign["q", i] = low_part(low, x, on_vector)

        def q_exp(i):
            nc.scalar.activation(out=q_work[i][:], in_=q_work[i][:], func=ACT.Exp, scale=sign["q", i])

        def q_map(i):
            if i < 0:
                e = q_work[i][:].rearrange("p (y r) -> p y r", r=2)
                nc.vector.scalar_tensor_tensor(out=e, in0=q_half(i), scalar=0.0, in1=e, op0=ALU.max, op1=ALU.add)
            else:
                nc.vector.tensor_scalar(
                    out=q_lin[i][:].rearrange("p j r s -> p j s r"),
                    in0=q_half(i).rearrange("p (j s) r -> p j s r", j=PACK),
                    scalar1=0.0,
                    scalar2=1.0,
                    op0=ALU.max,
                    op1=ALU.add,
                )

        def q_scale(i):
            for j in range(PACK):
                lin = q_lin[i][:, j, :, :].rearrange("p r s -> p (r s)")
                nc.scalar.activation(out=lin, in_=lin, func=ACT.Copy, scale=qa_sb[:, j : j + 1])

        def q_weigh(i):
            a, u = divmod(i, 2)
            dst = q_bf[a][:, 2 * u : 2 * u + 2, :, :]
            if i < 0:
                nc.vector.tensor_tensor(
                    out=dst.rearrange("p r s j -> p s j r"),
                    in0=q_work[i][:].rearrange("p (j s r) -> p s j r", j=PACK, r=2),
                    in1=qa_sb[:].unsqueeze(1).unsqueeze(3).to_broadcast([P, P, PACK, 2]),
                    op=ALU.mult,
                )
            else:
                nc.vector.tensor_tensor(
                    out=dst.rearrange("p r s j -> p (r s) j").rearrange("p (g w) j -> p g j w", w=2),
                    in0=q_work[i][:].rearrange("p (j g w) -> p g j w", j=PACK, w=2),
                    in1=q_lin[i][:].rearrange("p j r s -> p j (r s)").rearrange("p j (g w) -> p g j w", w=2),
                    op=ALU.mult,
                )

        def q_quant(i):
            a, u = divmod(i, 2)
            cols = slice(2 * P * u, 2 * P * (u + 1))
            quantize(
                q_codes[a][:, cols],
                q_scales[a][:, cols],
                q_bf[a][:, 2 * u : 2 * u + 2, :, :].rearrange("p r s j -> p (r s j)"),
            )

        def read_state(heads, rs):
            for r in rs:
                for h in heads:
                    a, c = divmod(h, PACK)
                    rows = slice(ROWS * c, ROWS * (c + 1))
                    nc.tensor.matmul_mx(
                        out=y_ps[h][:, r, :],
                        lhsT=q_codes[a][rows, P * r : P * (r + 1)].bitcast(FP8X4),
                        lhsT_scale=q_scales[a][rows, P * r : P * (r + 1)],
                        rhs=s_codes[a][rows, :].bitcast(FP8X4),
                        rhs_scale=s_scales[a][rows, :],
                        start=True,
                        stop=True,
                    )

        def gate_tanh(h):
            a, c = divmod(h, PACK)
            nc.scalar.activation(out=og_raw[a][:, c, :], in_=og_raw[a][:, c, :], func=ACT.Tanh, scale=0.5)

        def finish(h, parts=1):
            rows = PACK // parts
            gate = og_raw[h // PACK][:, h % PACK, :]
            for i in range(parts):
                cols = slice(i * rows * D, (i + 1) * rows * D)
                nc.vector.scalar_tensor_tensor(
                    out=gate[:, cols],
                    in0=gate[:, cols],
                    scalar=1.0,
                    in1=y_ps[h][:].rearrange("p r e -> p (r e)")[:, cols],
                    op0=ALU.add,
                    op1=ALU.mult,
                )
                nc.sync.dma_start(out=out[h].rearrange("(s r) e -> s (r e)", r=PACK)[:, cols], in_=gate[:, cols])

        k_low(0, True, cols=slice(0, N // 2))
        k_low(0, True, cols=slice(N // 2, N))
        k_exp(0, cols=slice(0, N // 2))
        weights()
        k_exp(0, cols=slice(N // 2, N))
        k_low(1)
        k_map(0, cols=slice(0, N // 2))
        k_map(0, cols=slice(N // 2, N))
        k_exp(1)
        k_low(2, True)
        k_weigh(0)
        k_low(3, True)
        k_exp(2)
        k_map(1)
        k_map(2)
        k_low(4)
        k_exp(3)
        k_weigh(1)
        k_map(3)
        k_exp(4)
        k_weigh(2)
        k_map(4)
        k_low(5)
        k_weigh(3)
        k_low(6)
        k_exp(5)
        k_map(5)
        k_weigh(4)
        k_quant(0)
        q_map(0)
        k_exp(6)
        v_round(0)
        q_low(0)
        q_low(1, True)
        v_round(1)
        k_move(0)
        v_round(2)
        k_weigh(5)
        q_scale(0)
        v_round(3)
        k_map(6)
        k_low(7, True)
        q_exp(0)
        v_quant(0)
        k_exp(7)
        q_map(1)
        q_weigh(0)
        q_low(2, True)
        q_map(2)
        q_exp(1)
        q_quant(0)
        v_round(4)
        k_weigh(6)
        q_scale(1)
        k_map(7)
        v_round(5)
        state(0)
        v_round(6)
        s_round(0)
        q_weigh(1)
        k_weigh(7)
        s_quant(0)
        read_state(range(4), (0, 1))
        q_quant(1)
        k_quant(1)
        v_round(7)
        read_state(range(4), (2, 3))
        v_quant(1)
        k_move(1)
        q_low(3, True)
        q_exp(2)
        gate_tanh(0)
        q_map(3)
        state(1)
        q_scale(2)
        gate_tanh(1)
        q_weigh(2)
        finish(0)
        q_exp(3)
        finish(1)
        q_quant(2)
        q_scale(3)
        q_weigh(3)
        s_round(1)
        s_quant(1)
        q_quant(3)
        read_state(range(4, 7), (0, 1))
        gate_tanh(2)
        gate_tanh(3)
        finish(2)
        gate_tanh(4)
        gate_tanh(5)
        gate_tanh(6)
        finish(3)
        read_state(range(4, 7), (2, 3))
        finish(4)
        finish(5)
        gate_tanh(7)
        read_state((7,), range(4))
        finish(6)
        finish(7, 2)
